import numpy as np
CORES = [0,8,16,24,32,40,48,56,64,72,80,88,96,104,112,120,128,136,144,152,160,168,176,184,192,200,208,216,224,232,240,248,256,264,272,280,288,296,304,312,320,328,336,344,352,360,368,376,384,392,400,408,416,424,432,440,448,456,464,472,480,488,496,504]
N = 64
T, W = 32, 8
ROUTE = [[46,38,24,32,16,40,41,39,52,46,33,32,7,35,42,32,44,39,10,22,45,6,0,46,10,17,32,61,8,44,37,23],[32,43,43,40,47,46,18,54,41,36,10,38,45,22,26,38,26,41,38,3,13,40,40,25,42,51,47,42,21,38,32,29],[32,40,0,22,42,38,36,44,45,42,40,46,32,26,33,29,7,21,34,33,32,36,57,44,34,3,35,34,27,36,39,49],[18,32,33,47,63,49,17,56,37,18,42,1,45,19,34,6,36,11,11,43,46,43,8,59,22,34,37,34,63,47,33,40],[37,61,33,34,31,14,46,13,44,36,58,32,47,63,45,48,37,8,32,34,47,41,45,53,41,17,33,40,11,33,48,20],[46,41,49,47,41,43,33,3,44,10,32,17,32,34,32,47,41,44,38,15,37,34,33,41,48,63,2,43,43,52,2,46],[36,16,32,63,39,36,44,33,58,35,8,10,45,41,40,38,51,16,18,54,15,2,2,46,23,40,46,33,49,43,47,27],[8,56,47,32,36,45,45,43,45,35,42,38,40,63,42,34,58,46,31,16,37,39,46,32,41,15,63,22,41,48,15,2],[41,46,41,34,45,44,38,40,12,0,18,52,37,41,47,30,46,32,0,36,44,6,44,54,1,44,46,44,56,34,34,52],[7,30,41,45,42,46,1,32,38,36,37,33,37,8,41,36,40,28,21,2,26,47,32,43,46,19,58,60,39,59,26,5],[39,12,24,36,16,32,37,46,6,54,34,9,22,34,7,47,41,42,39,36,47,19,62,43,34,7,32,47,26,44,46,39],[35,54,34,36,53,37,52,60,29,44,39,14,56,9,36,12,0,53,45,41,35,21,0,38,41,43,33,53,36,30,44,32],[55,46,39,58,53,11,47,54,37,16,35,49,4,37,42,51,36,33,51,35,42,15,33,34,39,35,32,46,46,44,63,56],[38,20,47,45,1,45,14,2,59,38,33,40,1,61,7,44,43,39,31,13,54,8,24,41,46,52,16,14,52,38,3,42],[55,60,42,10,41,43,23,31,10,38,33,36,36,15,16,32,52,53,35,43,10,20,47,34,52,40,43,23,38,52,20,60],[42,38,23,24,41,26,38,37,44,35,36,46,2,43,17,15,13,5,20,36,34,45,47,37,23,15,39,48,50,40,51,47],[40,38,6,50,4,63,48,32,11,40,41,25,57,28,38,46,42,39,42,47,2,40,56,17,9,46,30,52,38,45,47,39],[34,59,43,40,19,14,47,24,43,40,43,42,47,4,37,40,48,44,61,55,0,41,57,39,49,12,21,3,44,43,42,19],[6,62,37,38,41,42,42,39,43,52,44,6,44,48,43,33,40,62,33,34,41,45,41,26,62,46,28,22,23,34,37,39],[49,8,47,10,60,1,44,28,42,34,57,16,12,39,60,40,44,8,2,44,37,37,23,32,55,27,63,44,48,33,42,48],[2,38,32,16,44,3,56,41,40,40,46,1,59,27,40,7,57,4,45,32,33,36,10,46,57,47,39,3,44,47,33,36],[38,55,20,25,45,36,56,44,28,49,32,35,4,27,42,5,33,34,44,34,49,22,2,28,38,61,18,23,59,44,45,3],[45,9,47,39,47,39,46,36,35,13,47,39,52,55,39,33,9,35,13,45,39,33,12,5,34,47,34,44,43,47,36,43],[38,7,34,30,8,20,29,23,47,41,10,32,2,43,37,44,40,24,36,42,47,36,38,11,4,44,61,29,50,11,35,42],[26,48,47,29,29,38,41,39,46,44,32,52,55,56,52,42,39,44,59,40,47,47,45,32,17,34,46,61,32,60,63,33],[32,46,39,39,34,41,13,43,7,27,38,47,45,63,39,34,38,56,38,51,40,58,58,11,6,40,29,13,58,37,33,51],[37,37,47,36,33,29,39,46,42,17,60,16,8,61,39,47,42,2,16,40,41,4,39,15,41,17,39,50,37,35,34,35],[1,47,40,35,7,0,17,25,30,41,43,34,51,46,61,38,40,44,6,51,34,41,39,49,7,14,10,37,12,37,47,36],[37,63,2,47,44,37,48,28,47,3,34,32,60,17,37,34,46,46,53,9,38,47,43,38,61,32,33,46,44,43,14,48],[54,38,41,41,38,61,31,34,33,34,28,36,34,53,43,43,32,4,41,9,27,45,11,42,57,43,41,39,35,51,17,34],[20,45,32,15,40,4,36,42,38,39,39,44,1,10,39,37,28,43,41,38,28,41,56,32,41,38,26,10,43,12,52,16],[14,35,13,57,42,46,42,35,13,30,9,35,35,32,46,1,63,38,15,45,40,44,44,46,27,50,44,32,53,37,7,47],[40,33,37,36,42,11,40,6,44,53,44,7,40,45,32,36,33,35,47,47,43,34,34,38,47,48,32,35,20,37,5,29],[43,29,32,42,44,45,37,45,25,43,20,44,42,32,42,3,35,42,3,56,26,36,32,58,45,38,41,9,45,39,39,50],[34,15,46,30,45,52,46,26,41,56,37,38,34,45,32,45,37,45,40,8,32,54,45,20,45,32,47,25,55,34,7,31],[60,44,35,60,41,42,21,24,46,24,18,36,44,39,38,7,59,35,25,12,36,46,42,41,60,58,14,11,32,44,32,25],[45,47,17,59,37,48,35,8,46,34,8,36,38,36,46,45,50,17,0,42,33,5,35,61,33,4,56,36,40,8,43,35],[42,44,5,37,60,46,26,45,37,3,38,46,42,50,45,61,17,31,17,23,6,41,47,46,18,35,36,34,22,43,49,45],[42,35,32,49,52,47,44,46,5,38,30,3,48,13,41,0,36,45,45,39,12,52,41,44,37,38,38,50,32,8,31,46],[34,54,41,14,5,46,28,40,41,19,41,38,36,7,32,43,38,11,57,24,34,42,46,47,2,44,36,39,43,40,11,63],[46,7,34,39,17,36,32,34,46,34,40,43,9,43,36,34,42,41,35,47,3,39,53,36,16,43,11,35,51,39,34,26],[53,56,35,22,25,38,31,19,32,24,52,25,13,37,50,40,40,19,44,46,40,35,35,43,33,47,51,40,40,61,35,10],[34,45,57,32,28,47,3,13,37,48,34,41,34,59,31,49,44,37,58,33,33,45,36,41,61,32,14,4,38,60,40,43],[40,35,41,42,25,51,42,44,34,59,35,34,35,50,20,42,53,23,23,53,33,38,17,39,5,37,48,63,39,40,43,42],[51,39,46,41,34,46,2,41,4,28,41,42,39,55,51,49,46,26,63,46,41,38,26,29,25,38,0,30,52,31,61,19],[40,35,43,11,5,38,56,53,52,26,35,46,58,10,55,33,2,44,15,57,39,13,54,5,54,11,5,43,50,40,35,24],[44,45,32,46,41,43,3,32,21,63,18,55,43,26,37,12,34,44,48,12,38,45,40,51,34,33,46,48,4,35,10,2],[36,27,34,32,57,47,40,36,15,34,33,29,3,40,55,43,32,34,48,43,38,35,55,53,47,63,57,44,33,23,39,52],[40,48,46,36,34,50,42,47,4,7,43,37,59,0,39,39,0,42,4,39,32,26,43,38,46,46,9,47,35,10,9,35],[34,45,39,4,39,7,43,35,33,57,30,34,32,46,36,32,35,34,0,29,60,41,33,6,24,35,43,36,1,36,36,39],[32,36,51,34,32,47,47,51,9,10,40,44,22,39,36,5,10,39,27,41,53,43,38,45,39,17,9,32,28,46,60,32],[33,43,38,34,14,30,38,46,41,45,32,39,54,39,51,14,46,7,34,4,19,44,48,63,47,22,38,29,34,13,40,15],[43,42,40,13,47,34,1,3,38,38,18,35,61,44,47,47,29,46,40,61,59,37,46,35,28,38,35,21,35,40,10,21],[47,36,58,43,33,45,34,40,34,41,36,34,47,35,40,16,34,39,35,4,39,57,8,1,3,46,32,32,0,40,42,37],[33,34,52,50,30,20,42,30,35,54,32,0,44,32,31,28,54,36,3,21,36,40,46,14,36,56,43,36,34,22,36,39],[45,35,35,19,42,42,40,19,58,33,45,8,33,23,38,21,8,45,39,32,44,63,36,59,4,38,24,42,34,61,42,15],[57,7,15,59,58,32,44,38,43,59,11,39,39,6,44,22,38,45,41,63,33,36,41,47,47,36,41,58,40,32,32,34],[24,37,43,34,41,38,63,44,15,44,40,6,6,43,11,20,49,27,33,28,9,54,45,16,40,47,22,38,16,42,14,45],[44,16,43,15,40,9,12,47,47,19,32,49,42,35,12,31,32,36,15,39,37,13,13,61,28,36,34,38,44,10,55,29],[46,34,46,51,44,39,2,38,19,34,2,3,36,32,41,2,38,45,24,40,35,36,5,47,42,46,36,40,37,45,33,45],[21,40,19,39,40,46,24,33,46,41,54,25,47,37,45,33,39,23,51,43,42,16,41,27,3,41,0,47,38,47,53,18],[43,42,12,14,45,42,30,35,34,42,42,39,51,46,15,30,7,42,36,13,52,39,33,41,49,10,38,5,32,44,33,17],[39,24,40,54,38,43,33,47,57,44,62,30,21,27,46,53,52,10,39,47,54,36,2,33,9,32,4,41,56,40,38,30],[35,43,37,36,40,21,34,32,35,47,30,23,44,22,47,38,7,38,40,43,23,32,41,30,44,32,36,50,31,36,27,11]]
CAP = 90
def setup_inputs(rng):
    return {"x": rng.standard_normal((N, 128, T * W)).astype(np.float32)}
def reference(x):
    y = np.full((N, 128, CAP * W), np.nan, x.dtype)
    fill = [0] * N
    for r in range(N):
        for t in range(T):
            e = ROUTE[r][t]
            y[e][:, fill[e] * W:(fill[e] + 1) * W] = x[r][:, t * W:(t + 1) * W]
            fill[e] += 1
    return {"y": y}

@@ -1,0 +1,200 @@
+from concourse.bass import DstId, RemoteDMATransfer
+
+SCRATCH = {
+    "xs": ("sbuf", [128, 256], "float32"),
+    "land": ("sbuf", [128, 720], "float32"),
+}
+SEMAPHORES = ["loaded", "kept", "read", "arrived", "stored"]
+
+PLANS = {}
+
+
+def links_of(topo, a, b):
+    ha, ca, hb, cb, d = topo.host(a), topo.chip(a), topo.host(b), topo.chip(b), topo.die(a)
+    if (ha, ca) == (hb, cb):
+        return []
+    if topo.rack(ha) != topo.rack(hb):
+        if ca == cb:
+            return [("cable", ha, ca, (a % 8) // 2)]
+        return [("far-out", ha, ca, d), ("far-in", hb, cb, d)]
+    out = []
+    if (ca ^ cb) & 1:
+        out.append(("mate", ha, ca, d))
+        ca ^= 1
+    if (ha, ca) != (hb, cb):
+        out.append(("out", ha, ca, d))
+        out.append(("in", hb, cb, d))
+    return out
+
+
+def build_plan(route, cores, topo):
+    n = len(cores)
+    host = [topo.host(c) for c in cores]
+    chip = [topo.chip(c) for c in cores]
+    tokens, fill = [], [0] * n
+    for r in range(n):
+        for t, e in enumerate(route[r]):
+            tokens.append((r, t, e, fill[e]))
+            fill[e] += 1
+
+    def at(h, c, k):
+        return (h * 16 + c) * 8 + k
+
+    enter = [0] * 4
+    for r, t, e, p in tokens:
+        if host[r] != host[e]:
+            enter[host[e]] += 1
+    hot = max(range(4), key=lambda h: enter[h])
+    pair = {}
+    via = {}
+    for i, (r, t, e, p) in enumerate(tokens):
+        h, h2 = host[r], host[e]
+        if topo.rack(h) == topo.rack(h2):
+            continue
+        if h ^ h2 != 2:
+            key = (h, h2)
+        elif 3 - h != hot:
+            via[i] = 3 - h
+            key = (h, 3 - h)
+        else:
+            via[i] = h ^ 1
+            key = (h ^ 1, h2)
+        pair[key] = pair.get(key, 0) + 1
+    for h in range(4):
+        if hot in (h ^ 1, 3 - h):
+            continue
+        first, other = (h, 3 - h), (h ^ 1, h ^ 2)
+        on_cable, turned = {}, {}
+        free = []
+        for i in via:
+            r, t, e, p = tokens[i]
+            if host[r] == h:
+                on_cable[r] = on_cable.get(r, 0) + 1
+                if (chip[r] ^ chip[e]) & 1 == 0:
+                    free.append(i)
+        while free and pair.get(first, 0) - pair.get(other, 0) >= 2:
+            i = min(free, key=lambda j: (-on_cable[tokens[j][0]], turned.get(tokens[j][2], 0), j))
+            free.remove(i)
+            via[i] = h ^ 1
+            on_cable[tokens[i][0]] -= 1
+            turned[tokens[i][2]] = turned.get(tokens[i][2], 0) + 1
+            pair[first] -= 1
+            pair[other] = pair.get(other, 0) + 1
+
+    def options(i):
+        r, t, e, p = tokens[i]
+        h, c, c2 = host[r], chip[r], chip[e]
+        turn = (c ^ c2) & 1
+        ks = (2, 3, 6, 7) if turn else (1, 2, 3, 4, 5, 6, 7)
+        if i in via:
+            v = via[i]
+            mid = c if v == 3 - h else c2 ^ turn
+            return [(cores[r], at(v, mid, k), cores[e]) for k in ks]
+        own = [(cores[r], at(h, c, k), cores[e]) for k in ks]
+        return own if turn else [(cores[r], cores[e])] + own
+
+    load, busy = {}, {}
+
+    def path_links(path):
+        out = []
+        for a, b in zip(path, path[1:]):
+            out += links_of(topo, a, b)
+        return out
+
+    def price(path):
+        c = 0.0
+        for l in path_links(path):
+            c += 2 * load.get(l, 0) + 1
+        if len(path) == 3:
+            c += 0.5 + 0.01 * (2 * busy.get(path[1], 0) + 1)
+        return c
+
+    def book(path, s):
+        for l in path_links(path):
+            load[l] = load.get(l, 0) + s
+        if len(path) == 3:
+            busy[path[1]] = busy.get(path[1], 0) + s
+
+    moving = [i for i in range(len(tokens)) if tokens[i][0] != tokens[i][2]]
+    opts = {i: options(i) for i in moving}
+    path = {}
+    for sweep in range(30):
+        changed = 0
+        for i in moving:
+            if i in path:
+                book(path[i], -1)
+            best = min(opts[i], key=price)
+            if path.get(i) != best:
+                changed += 1
+            path[i] = best
+            book(best, 1)
+        if not changed:
+            break
+
+    plan = {}
+
+    def prog(c):
+        if c not in plan:
+            plan[c] = {"sends": [], "arrive": 0, "kept": [], "count": 0, "slots": 0}
+        return plan[c]
+
+    for r in range(n):
+        prog(cores[r])["count"] = fill[r]
+    for i, (r, t, e, p) in enumerate(tokens):
+        if r == e:
+            prog(cores[r])["kept"].append((t, p))
+            continue
+        way = path[i]
+        if len(way) == 3:
+            mid = prog(way[1])
+            slot = mid["slots"]
+            mid["slots"] += 1
+            mid["arrive"] += 1
+            prog(way[0])["sends"].append((t, way[1], slot))
+            mid["sends"].append((slot, way[2], p))
+        else:
+            prog(way[0])["sends"].append((t, way[1], p))
+        prog(way[-1])["arrive"] += 1
+    return plan
+
+
+def send_all(g, core, T, topo, src, sends, w):
+    far = [s for s in sends if s[1] // 8 != core // 8]
+    near = [s for s in sends if s[1] // 8 == core // 8]
+    ncalls = max((len(far) + 7) // 8, (len(sends) + 15) // 16)
+    calls = [far[j::ncalls] for j in range(ncalls)]
+    for s in near:
+        min(calls, key=len).append(s)
+    for call in calls:
+        transfers = []
+        for engine, (slot, dst, dslot) in enumerate(call):
+            rid, pid = topo.addr(dst, core)
+            transfers.append(RemoteDMATransfer(
+                dst_ids=[DstId(rid=rid, pnc=pid)], dma_engine_mask=1 << engine, remote_sem=T.sem.arrived,
+                src=src[:, slot * w:(slot + 1) * w], dst=T.land[:, dslot * w:(dslot + 1) * w]))
+        g.remote_dma_fused(transfers, local_sem=T.sem.read)
+    return len(sends)
+
+
+def rank_program(g, core, T, topo):
+    if "plan" not in PLANS:
+        PLANS["plan"] = build_plan(T.tables["ROUTE"], list(T.cores), topo)
+    me = PLANS["plan"].get(core)
+    if me is None:
+        return
+    w = T.tables["W"]
+    if T.rank_of(core) is None:
+        g.wait_ge(T.sem.arrived, me["arrive"])
+        g.wait_ge(T.sem.read, send_all(g, core, T, topo, T.land, me["sends"], w))
+        return
+    g.dma_start(T.xs[:], T.x[:]).then_inc(T.sem.loaded, 16)
+    for t, p in me["kept"]:
+        g.dma_start(T.land[:, p * w:(p + 1) * w], T.x[:, t * w:(t + 1) * w]).then_inc(T.sem.kept, 16)
+    g.wait_ge(T.sem.loaded, 16)
+    sent = send_all(g, core, T, topo, T.xs, me["sends"], w)
+    g.wait_ge(T.sem.arrived, me["arrive"])
+    if me["kept"]:
+        g.wait_ge(T.sem.kept, 16 * len(me["kept"]))
+    g.dma_start(T.y[:, :me["count"] * w], T.land[:, :me["count"] * w]).then_inc(T.sem.stored, 16)
+    g.wait_ge(T.sem.stored, 16)
+    g.wait_ge(T.sem.read, sent)

@@ -1,10 +1,12 @@
 from concourse.bass import DstId, RemoteDMATransfer
 
+BLOCK = 4
+RACK_FIRST_RELAYS = (1, 4)
 SCRATCH = {
     "xs": ("sbuf", [128, 256], "float32"),
     "land": ("sbuf", [128, 720], "float32"),
 }
-SEMAPHORES = ["loaded", "kept", "read", "arrived", "stored"]
+SEMAPHORES = ["loaded", "kept", "handed", "arrived", "read", "stored"]
 
 PLANS = {}
 
@@ -27,6 +29,176 @@ def links_of(topo, a, b):
     return out
 
 
+def pack(sends, engines):
+    ncalls = (len(sends) + engines - 1) // engines
+    calls = []
+    for j in range(ncalls):
+        call = sends[j::ncalls]
+        per = 1
+        while 2 * per * len(call) <= engines:
+            per *= 2
+        calls.append([(s, per, ((1 << per) - 1) << (per * q)) for q, s in enumerate(call)])
+    return calls
+
+
+def add(d, k, v):
+    d[k] = d.get(k, 0) + v
+
+
+def choose_ways(tokens, cores, host, chip, topo):
+    enter = [0] * 4
+    for r, t, e, p in tokens:
+        if host[r] != host[e]:
+            enter[host[e]] += 1
+    hot = max(range(4), key=lambda h: enter[h])
+    via = {}
+    pair = {}
+    sends = {}
+    ingress = {}
+    for i, (r, t, e, p) in enumerate(tokens):
+        h, h2 = host[r], host[e]
+        if r != e:
+            add(sends, (h, chip[r]), 1)
+        if topo.rack(h) == topo.rack(h2):
+            if r != e and not topo.mates(cores[r], cores[e]):
+                add(ingress, e, 1)
+        elif h ^ h2 != 2:
+            add(pair, (h, h2), 1)
+        elif 3 - h != hot:
+            via[i] = 3 - h
+            add(pair, (h, 3 - h), 1)
+            add(sends, (3 - h, chip[r]), 1)
+            add(ingress, e, 1)
+        else:
+            via[i] = h ^ 1
+            add(pair, (h ^ 1, h2), 1)
+            add(sends, (h ^ 1, chip[e]), 1)
+    for h in range(4):
+        if hot in (h ^ 1, 3 - h):
+            continue
+        first, other = (h, 3 - h), (h ^ 1, h ^ 2)
+        free = [i for i in via if host[tokens[i][0]] == h]
+
+        def relieved(j):
+            return sends[(3 - h, chip[tokens[j][0]])]
+
+        def rank_of_turn(j):
+            r, t, e, p = tokens[j]
+            return (-relieved(j), 1 - ((chip[r] ^ chip[e]) & 1), -ingress[e], j)
+
+        while pair.get(first, 0) - pair.get(other, 0) >= 2:
+            ok = [j for j in free if sends.get((h ^ 1, chip[tokens[j][2]]), 0) < relieved(j)]
+            if not ok:
+                break
+            i = min(ok, key=rank_of_turn)
+            free.remove(i)
+            r, t, e, p = tokens[i]
+            via[i] = h ^ 1
+            add(sends, (3 - h, chip[r]), -1)
+            add(sends, (h ^ 1, chip[e]), 1)
+            add(ingress, e, -1)
+            add(pair, first, -1)
+            add(pair, other, 1)
+    return via
+
+
+def choose_cores(tokens, via, cores, host, chip, topo):
+    def at(h, c, k):
+        return (h * 16 + c) * 8 + k
+
+    rack_first_hosts = [v for i, v in via.items() if v == host[tokens[i][0]] ^ 1]
+    target = {}
+    relay_opts = {}
+    blocks = {}
+    for i, (r, t, e, p) in enumerate(tokens):
+        if r == e:
+            continue
+        blocks.setdefault((r, t // BLOCK), []).append(i)
+        target[i] = cores[e]
+        if i in via:
+            v = via[i]
+            if v == host[r] ^ 1:
+                mid, ks = chip[e], RACK_FIRST_RELAYS
+            else:
+                mid, ks = chip[r], [k for k in range(1, 8) if not (v in rack_first_hosts and k in RACK_FIRST_RELAYS)]
+            target[i] = at(v, mid, 0)
+            relay_opts[i] = [at(v, mid, k) for k in ks if topo.may_write(at(v, mid, k), cores[e])]
+    helper_opts = {}
+    for (r, b), its in blocks.items():
+        helper_opts[(r, b)] = [cores[r] + k for k in range(1, 8)
+                               if all(topo.may_write(cores[r] + k, target[i]) for i in its)]
+
+    load, busy, held = {}, {}, {}
+
+    def price(links, core, writes):
+        count = {}
+        for l in links:
+            add(count, l, 1)
+        c = 0
+        for l, m in count.items():
+            c += (3 if l[0] == "cable" else 1) * m * (2 * load.get(l, 0) + m)
+        return c + writes * (2 * busy.get(core, 0) + writes)
+
+    def book(links, core, writes, sign):
+        for l in links:
+            add(load, l, sign)
+        add(busy, core, sign * writes)
+
+    def block_links(key, k):
+        out = []
+        for i in blocks[key]:
+            out += links_of(topo, k, target[i])
+        return out
+
+    def place(key, k, sign):
+        book(block_links(key, k), k, len(blocks[key]), sign)
+        add(held, k, sign)
+
+    def block_price(key, k):
+        return price(block_links(key, k), k, len(blocks[key]))
+
+    helper, relay = {}, {}
+    keys = list(blocks)
+    for sweep in range(40):
+        changed = 0
+        for key in keys:
+            if key in helper:
+                place(key, helper[key], -1)
+            best = min([k for k in helper_opts[key] if held.get(k, 0) * BLOCK < 8], key=lambda k: block_price(key, k))
+            changed += helper.get(key) != best
+            helper[key] = best
+            place(key, best, 1)
+        for a in keys:
+            for b in keys:
+                ka, kb = helper[a], helper[b]
+                if a[0] != b[0] or a[1] >= b[1] or ka == kb or kb not in helper_opts[a] or ka not in helper_opts[b]:
+                    continue
+                place(a, ka, -1)
+                place(b, kb, -1)
+                cost = []
+                for xa, xb in ((ka, kb), (kb, ka)):
+                    c = block_price(a, xa)
+                    place(a, xa, 1)
+                    cost.append(c + block_price(b, xb))
+                    place(a, xa, -1)
+                if cost[1] < cost[0]:
+                    helper[a], helper[b] = kb, ka
+                    changed += 1
+                place(a, helper[a], 1)
+                place(b, helper[b], 1)
+        for i, opts in relay_opts.items():
+            e = cores[tokens[i][2]]
+            if i in relay:
+                book(links_of(topo, relay[i], e), relay[i], 1, -1)
+            best = min(opts, key=lambda j: price(links_of(topo, j, e), j, 1))
+            changed += relay.get(i) != best
+            relay[i] = best
+            book(links_of(topo, best, e), best, 1, 1)
+        if not changed:
+            break
+    return helper, relay
+
+
 def build_plan(route, cores, topo):
     n = len(cores)
     host = [topo.host(c) for c in cores]
@@ -36,144 +208,52 @@ def build_plan(route, cores, topo):
         for t, e in enumerate(route[r]):
             tokens.append((r, t, e, fill[e]))
             fill[e] += 1
-
-    def at(h, c, k):
-        return (h * 16 + c) * 8 + k
-
-    enter = [0] * 4
-    for r, t, e, p in tokens:
-        if host[r] != host[e]:
-            enter[host[e]] += 1
-    hot = max(range(4), key=lambda h: enter[h])
-    pair = {}
-    via = {}
-    for i, (r, t, e, p) in enumerate(tokens):
-        h, h2 = host[r], host[e]
-        if topo.rack(h) == topo.rack(h2):
-            continue
-        if h ^ h2 != 2:
-            key = (h, h2)
-        elif 3 - h != hot:
-            via[i] = 3 - h
-            key = (h, 3 - h)
-        else:
-            via[i] = h ^ 1
-            key = (h ^ 1, h2)
-        pair[key] = pair.get(key, 0) + 1
-    for h in range(4):
-        if hot in (h ^ 1, 3 - h):
-            continue
-        first, other = (h, 3 - h), (h ^ 1, h ^ 2)
-        on_cable, turned = {}, {}
-        free = []
-        for i in via:
-            r, t, e, p = tokens[i]
-            if host[r] == h:
-                on_cable[r] = on_cable.get(r, 0) + 1
-                if (chip[r] ^ chip[e]) & 1 == 0:
-                    free.append(i)
-        while free and pair.get(first, 0) - pair.get(other, 0) >= 2:
-            i = min(free, key=lambda j: (-on_cable[tokens[j][0]], turned.get(tokens[j][2], 0), j))
-            free.remove(i)
-            via[i] = h ^ 1
-            on_cable[tokens[i][0]] -= 1
-            turned[tokens[i][2]] = turned.get(tokens[i][2], 0) + 1
-            pair[first] -= 1
-            pair[other] = pair.get(other, 0) + 1
-
-    def options(i):
-        r, t, e, p = tokens[i]
-        h, c, c2 = host[r], chip[r], chip[e]
-        turn = (c ^ c2) & 1
-        ks = (2, 3, 6, 7) if turn else (1, 2, 3, 4, 5, 6, 7)
-        if i in via:
-            v = via[i]
-            mid = c if v == 3 - h else c2 ^ turn
-            return [(cores[r], at(v, mid, k), cores[e]) for k in ks]
-        own = [(cores[r], at(h, c, k), cores[e]) for k in ks]
-        return own if turn else [(cores[r], cores[e])] + own
-
-    load, busy = {}, {}
-
-    def path_links(path):
-        out = []
-        for a, b in zip(path, path[1:]):
-            out += links_of(topo, a, b)
-        return out
-
-    def price(path):
-        c = 0.0
-        for l in path_links(path):
-            c += 2 * load.get(l, 0) + 1
-        if len(path) == 3:
-            c += 0.5 + 0.01 * (2 * busy.get(path[1], 0) + 1)
-        return c
-
-    def book(path, s):
-        for l in path_links(path):
-            load[l] = load.get(l, 0) + s
-        if len(path) == 3:
-            busy[path[1]] = busy.get(path[1], 0) + s
-
-    moving = [i for i in range(len(tokens)) if tokens[i][0] != tokens[i][2]]
-    opts = {i: options(i) for i in moving}
-    path = {}
-    for sweep in range(30):
-        changed = 0
-        for i in moving:
-            if i in path:
-                book(path[i], -1)
-            best = min(opts[i], key=price)
-            if path.get(i) != best:
-                changed += 1
-            path[i] = best
-            book(best, 1)
-        if not changed:
-            break
+    via = choose_ways(tokens, cores, host, chip, topo)
+    helper, relay = choose_cores(tokens, via, cores, host, chip, topo)
 
     plan = {}
 
     def prog(c):
         if c not in plan:
-            plan[c] = {"sends": [], "arrive": 0, "kept": [], "count": 0, "slots": 0}
+            plan[c] = {"blocks": [], "own": [], "pass": [], "handed": 0, "arrived": 0, "kept": [], "count": 0}
         return plan[c]
 
     for r in range(n):
         prog(cores[r])["count"] = fill[r]
+    for (r, b), k in helper.items():
+        prog(cores[r])["blocks"].append((b * BLOCK, k, b * BLOCK))
     for i, (r, t, e, p) in enumerate(tokens):
         if r == e:
             prog(cores[r])["kept"].append((t, p))
             continue
-        way = path[i]
-        if len(way) == 3:
-            mid = prog(way[1])
-            slot = mid["slots"]
-            mid["slots"] += 1
-            mid["arrive"] += 1
-            prog(way[0])["sends"].append((t, way[1], slot))
-            mid["sends"].append((slot, way[2], p))
+        mine = prog(helper[(r, t // BLOCK)])["own"]
+        if i in relay:
+            passing = prog(relay[i])["pass"]
+            mine.append((t, relay[i], len(passing)))
+            passing.append((len(passing), cores[e], p))
         else:
-            prog(way[0])["sends"].append((t, way[1], p))
-        prog(way[-1])["arrive"] += 1
+            mine.append((t, cores[e], p))
+    for c in list(plan):
+        for kind, engines, sem in (("blocks", 16, "handed"), ("own", 8, "arrived"), ("pass", 8, "arrived")):
+            for call in pack(plan[c][kind], engines):
+                for (slot, dst, dslot), per, mask in call:
+                    plan[dst][sem] += per
     return plan
 
 
-def send_all(g, core, T, topo, src, sends, w):
-    far = [s for s in sends if s[1] // 8 != core // 8]
-    near = [s for s in sends if s[1] // 8 == core // 8]
-    ncalls = max((len(far) + 7) // 8, (len(sends) + 15) // 16)
-    calls = [far[j::ncalls] for j in range(ncalls)]
-    for s in near:
-        min(calls, key=len).append(s)
-    for call in calls:
+def send(g, core, T, topo, sends, engines, src, dst, sem, width):
+    w = T.tables["W"]
+    total = 0
+    for call in pack(sends, engines):
         transfers = []
-        for engine, (slot, dst, dslot) in enumerate(call):
-            rid, pid = topo.addr(dst, core)
+        for (slot, to, dslot), per, mask in call:
+            rid, pid = topo.addr(to, core)
             transfers.append(RemoteDMATransfer(
-                dst_ids=[DstId(rid=rid, pnc=pid)], dma_engine_mask=1 << engine, remote_sem=T.sem.arrived,
-                src=src[:, slot * w:(slot + 1) * w], dst=T.land[:, dslot * w:(dslot + 1) * w]))
+                dst_ids=[DstId(rid=rid, pnc=pid)], dma_engine_mask=mask, remote_sem=sem,
+                src=src[:, slot * w:slot * w + width], dst=dst[:, dslot * w:dslot * w + width]))
+            total += per
         g.remote_dma_fused(transfers, local_sem=T.sem.read)
-    return len(sends)
+    return total
 
 
 def rank_program(g, core, T, topo):
@@ -184,17 +264,23 @@ def rank_program(g, core, T, topo):
         return
     w = T.tables["W"]
     if T.rank_of(core) is None:
-        g.wait_ge(T.sem.arrived, me["arrive"])
-        g.wait_ge(T.sem.read, send_all(g, core, T, topo, T.land, me["sends"], w))
+        left = 0
+        if me["own"]:
+            g.wait_ge(T.sem.handed, me["handed"])
+            left += send(g, core, T, topo, me["own"], 8, T.xs, T.land, T.sem.arrived, w)
+        if me["pass"]:
+            g.wait_ge(T.sem.arrived, me["arrived"])
+            left += send(g, core, T, topo, me["pass"], 8, T.land, T.land, T.sem.arrived, w)
+        g.wait_ge(T.sem.read, left)
         return
     g.dma_start(T.xs[:], T.x[:]).then_inc(T.sem.loaded, 16)
     for t, p in me["kept"]:
         g.dma_start(T.land[:, p * w:(p + 1) * w], T.x[:, t * w:(t + 1) * w]).then_inc(T.sem.kept, 16)
     g.wait_ge(T.sem.loaded, 16)
-    sent = send_all(g, core, T, topo, T.xs, me["sends"], w)
-    g.wait_ge(T.sem.arrived, me["arrive"])
+    left = send(g, core, T, topo, me["blocks"], 16, T.xs, T.xs, T.sem.handed, BLOCK * w)
+    g.wait_ge(T.sem.arrived, me["arrived"])
     if me["kept"]:
         g.wait_ge(T.sem.kept, 16 * len(me["kept"]))
     g.dma_start(T.y[:, :me["count"] * w], T.land[:, :me["count"] * w]).then_inc(T.sem.stored, 16)
     g.wait_ge(T.sem.stored, 16)
-    g.wait_ge(T.sem.read, sent)
+    g.wait_ge(T.sem.read, left)

@@ -3,8 +3,8 @@ from concourse.bass import DstId, RemoteDMATransfer
 BLOCK = 4
 RACK_FIRST_RELAYS = (1, 4)
 SCRATCH = {
-    "xs": ("sbuf", [128, 256], "float32"),
-    "land": ("sbuf", [128, 720], "float32"),
+    "xs": ("sbuf", [128, 32, 8], "float32"),
+    "land": ("sbuf", [128, 90, 8], "float32"),
 }
 SEMAPHORES = ["loaded", "kept", "handed", "arrived", "read", "stored"]
 
@@ -39,6 +39,18 @@ def pack(sends, engines):
             per *= 2
         calls.append([(s, per, ((1 << per) - 1) << (per * q)) for q, s in enumerate(call)])
     return calls
+
+
+def spaced_runs(kept):
+    runs = []
+    for t, p in kept:
+        if runs:
+            t0, step, m, p0 = runs[-1]
+            if m == 1 or t == t0 + step * m:
+                runs[-1] = (t0, t - t0 if m == 1 else step, m + 1, p0)
+                continue
+        runs.append((t, 1, 1, p))
+    return runs
 
 
 def add(d, k, v):
@@ -242,7 +254,6 @@ def build_plan(route, cores, topo):
 
 
 def send(g, core, T, topo, sends, engines, src, dst, sem, width):
-    w = T.tables["W"]
     total = 0
     for call in pack(sends, engines):
         transfers = []
@@ -250,7 +261,7 @@ def send(g, core, T, topo, sends, engines, src, dst, sem, width):
             rid, pid = topo.addr(to, core)
             transfers.append(RemoteDMATransfer(
                 dst_ids=[DstId(rid=rid, pnc=pid)], dma_engine_mask=mask, remote_sem=sem,
-                src=src[:, slot * w:slot * w + width], dst=dst[:, dslot * w:dslot * w + width]))
+                src=src[:, slot:slot + width, :], dst=dst[:, dslot:dslot + width, :]))
             total += per
         g.remote_dma_fused(transfers, local_sem=T.sem.read)
     return total
@@ -262,25 +273,25 @@ def rank_program(g, core, T, topo):
     me = PLANS["plan"].get(core)
     if me is None:
         return
-    w = T.tables["W"]
     if T.rank_of(core) is None:
         left = 0
         if me["own"]:
             g.wait_ge(T.sem.handed, me["handed"])
-            left += send(g, core, T, topo, me["own"], 8, T.xs, T.land, T.sem.arrived, w)
+            left += send(g, core, T, topo, me["own"], 8, T.xs, T.land, T.sem.arrived, 1)
         if me["pass"]:
             g.wait_ge(T.sem.arrived, me["arrived"])
-            left += send(g, core, T, topo, me["pass"], 8, T.land, T.land, T.sem.arrived, w)
+            left += send(g, core, T, topo, me["pass"], 8, T.land, T.land, T.sem.arrived, 1)
         g.wait_ge(T.sem.read, left)
         return
     g.dma_start(T.xs[:], T.x[:]).then_inc(T.sem.loaded, 16)
-    for t, p in me["kept"]:
-        g.dma_start(T.land[:, p * w:(p + 1) * w], T.x[:, t * w:(t + 1) * w]).then_inc(T.sem.kept, 16)
     g.wait_ge(T.sem.loaded, 16)
-    left = send(g, core, T, topo, me["blocks"], 16, T.xs, T.xs, T.sem.handed, BLOCK * w)
+    left = send(g, core, T, topo, me["blocks"], 16, T.xs, T.xs, T.sem.handed, BLOCK)
+    runs = spaced_runs(me["kept"])
+    for t, step, m, p in runs:
+        g.dma_start(T.land[:, p:p + m, :], T.xs[:, t:t + step * (m - 1) + 1:step, :]).then_inc(T.sem.kept, 16)
     g.wait_ge(T.sem.arrived, me["arrived"])
-    if me["kept"]:
-        g.wait_ge(T.sem.kept, 16 * len(me["kept"]))
-    g.dma_start(T.y[:, :me["count"] * w], T.land[:, :me["count"] * w]).then_inc(T.sem.stored, 16)
+    if runs:
+        g.wait_ge(T.sem.kept, 16 * len(runs))
+    g.dma_start(T.y[:, :me["count"] * T.tables["W"]], T.land[:, :me["count"], :]).then_inc(T.sem.stored, 16)
     g.wait_ge(T.sem.stored, 16)
     g.wait_ge(T.sem.read, left)

@@ -94,7 +94,7 @@ def choose_ways(tokens, cores, host, chip, topo):
         def relieved(j):
             return sends[(3 - h, chip[tokens[j][0]])]
 
-        def rank_of_turn(j):
+        def turn_order(j):
             r, t, e, p = tokens[j]
             return (-relieved(j), 1 - ((chip[r] ^ chip[e]) & 1), -ingress[e], j)
 
@@ -102,7 +102,7 @@ def choose_ways(tokens, cores, host, chip, topo):
             ok = [j for j in free if sends.get((h ^ 1, chip[tokens[j][2]]), 0) < relieved(j)]
             if not ok:
                 break
-            i = min(ok, key=rank_of_turn)
+            i = min(ok, key=turn_order)
             free.remove(i)
             r, t, e, p = tokens[i]
             via[i] = h ^ 1

from concourse.bass import DstId, RemoteDMATransfer

BLOCK = 4
RACK_FIRST_RELAYS = (1, 4)
SCRATCH = {
    "xs": ("sbuf", [128, 32, 8], "float32"),
    "land": ("sbuf", [128, 90, 8], "float32"),
}
SEMAPHORES = ["loaded", "kept", "handed", "arrived", "read", "stored"]

PLANS = {}


def links_of(topo, a, b):
    ha, ca, hb, cb, d = topo.host(a), topo.chip(a), topo.host(b), topo.chip(b), topo.die(a)
    if (ha, ca) == (hb, cb):
        return []
    if topo.rack(ha) != topo.rack(hb):
        if ca == cb:
            return [("cable", ha, ca, (a % 8) // 2)]
        return [("far-out", ha, ca, d), ("far-in", hb, cb, d)]
    out = []
    if (ca ^ cb) & 1:
        out.append(("mate", ha, ca, d))
        ca ^= 1
    if (ha, ca) != (hb, cb):
        out.append(("out", ha, ca, d))
        out.append(("in", hb, cb, d))
    return out


def pack(sends, engines):
    ncalls = (len(sends) + engines - 1) // engines
    calls = []
    for j in range(ncalls):
        call = sends[j::ncalls]
        per = 1
        while 2 * per * len(call) <= engines:
            per *= 2
        calls.append([(s, per, ((1 << per) - 1) << (per * q)) for q, s in enumerate(call)])
    return calls


def spaced_runs(kept):
    runs = []
    for t, p in kept:
        if runs:
            t0, step, m, p0 = runs[-1]
            if m == 1 or t == t0 + step * m:
                runs[-1] = (t0, t - t0 if m == 1 else step, m + 1, p0)
                continue
        runs.append((t, 1, 1, p))
    return runs


def add(d, k, v):
    d[k] = d.get(k, 0) + v


def choose_ways(tokens, cores, host, chip, topo):
    enter = [0] * 4
    for r, t, e, p in tokens:
        if host[r] != host[e]:
            enter[host[e]] += 1
    hot = max(range(4), key=lambda h: enter[h])
    via = {}
    pair = {}
    sends = {}
    ingress = {}
    for i, (r, t, e, p) in enumerate(tokens):
        h, h2 = host[r], host[e]
        if r != e:
            add(sends, (h, chip[r]), 1)
        if topo.rack(h) == topo.rack(h2):
            if r != e and not topo.mates(cores[r], cores[e]):
                add(ingress, e, 1)
        elif h ^ h2 != 2:
            add(pair, (h, h2), 1)
        elif 3 - h != hot:
            via[i] = 3 - h
            add(pair, (h, 3 - h), 1)
            add(sends, (3 - h, chip[r]), 1)
            add(ingress, e, 1)
        else:
            via[i] = h ^ 1
            add(pair, (h ^ 1, h2), 1)
            add(sends, (h ^ 1, chip[e]), 1)
    for h in range(4):
        if hot in (h ^ 1, 3 - h):
            continue
        first, other = (h, 3 - h), (h ^ 1, h ^ 2)
        free = [i for i in via if host[tokens[i][0]] == h]

        def relieved(j):
            return sends[(3 - h, chip[tokens[j][0]])]

        def turn_order(j):
            r, t, e, p = tokens[j]
            return (-relieved(j), 1 - ((chip[r] ^ chip[e]) & 1), -ingress[e], j)

        while pair.get(first, 0) - pair.get(other, 0) >= 2:
            ok = [j for j in free if sends.get((h ^ 1, chip[tokens[j][2]]), 0) < relieved(j)]
            if not ok:
                break
            i = min(ok, key=turn_order)
            free.remove(i)
            r, t, e, p = tokens[i]
            via[i] = h ^ 1
            add(sends, (3 - h, chip[r]), -1)
            add(sends, (h ^ 1, chip[e]), 1)
            add(ingress, e, -1)
            add(pair, first, -1)
            add(pair, other, 1)
    return via


def choose_cores(tokens, via, cores, host, chip, topo):
    def at(h, c, k):
        return (h * 16 + c) * 8 + k

    rack_first_hosts = [v for i, v in via.items() if v == host[tokens[i][0]] ^ 1]
    target = {}
    relay_opts = {}
    blocks = {}
    for i, (r, t, e, p) in enumerate(tokens):
        if r == e:
            continue
        blocks.setdefault((r, t // BLOCK), []).append(i)
        target[i] = cores[e]
        if i in via:
            v = via[i]
            if v == host[r] ^ 1:
                mid, ks = chip[e], RACK_FIRST_RELAYS
            else:
                mid, ks = chip[r], [k for k in range(1, 8) if not (v in rack_first_hosts and k in RACK_FIRST_RELAYS)]
            target[i] = at(v, mid, 0)
            relay_opts[i] = [at(v, mid, k) for k in ks if topo.may_write(at(v, mid, k), cores[e])]
    helper_opts = {}
    for (r, b), its in blocks.items():
        helper_opts[(r, b)] = [cores[r] + k for k in range(1, 8)
                               if all(topo.may_write(cores[r] + k, target[i]) for i in its)]

    load, busy, held = {}, {}, {}

    def price(links, core, writes):
        count = {}
        for l in links:
            add(count, l, 1)
        c = 0
        for l, m in count.items():
            c += (3 if l[0] == "cable" else 1) * m * (2 * load.get(l, 0) + m)
        return c + writes * (2 * busy.get(core, 0) + writes)

    def book(links, core, writes, sign):
        for l in links:
            add(load, l, sign)
        add(busy, core, sign * writes)

    def block_links(key, k):
        out = []
        for i in blocks[key]:
            out += links_of(topo, k, target[i])
        return out

    def place(key, k, sign):
        book(block_links(key, k), k, len(blocks[key]), sign)
        add(held, k, sign)

    def block_price(key, k):
        return price(block_links(key, k), k, len(blocks[key]))

    helper, relay = {}, {}
    keys = list(blocks)
    for sweep in range(40):
        changed = 0
        for key in keys:
            if key in helper:
                place(key, helper[key], -1)
            best = min([k for k in helper_opts[key] if held.get(k, 0) * BLOCK < 8], key=lambda k: block_price(key, k))
            changed += helper.get(key) != best
            helper[key] = best
            place(key, best, 1)
        for a in keys:
            for b in keys:
                ka, kb = helper[a], helper[b]
                if a[0] != b[0] or a[1] >= b[1] or ka == kb or kb not in helper_opts[a] or ka not in helper_opts[b]:
                    continue
                place(a, ka, -1)
                place(b, kb, -1)
                cost = []
                for xa, xb in ((ka, kb), (kb, ka)):
                    c = block_price(a, xa)
                    place(a, xa, 1)
                    cost.append(c + block_price(b, xb))
                    place(a, xa, -1)
                if cost[1] < cost[0]:
                    helper[a], helper[b] = kb, ka
                    changed += 1
                place(a, helper[a], 1)
                place(b, helper[b], 1)
        for i, opts in relay_opts.items():
            e = cores[tokens[i][2]]
            if i in relay:
                book(links_of(topo, relay[i], e), relay[i], 1, -1)
            best = min(opts, key=lambda j: price(links_of(topo, j, e), j, 1))
            changed += relay.get(i) != best
            relay[i] = best
            book(links_of(topo, best, e), best, 1, 1)
        if not changed:
            break
    return helper, relay


def build_plan(route, cores, topo):
    n = len(cores)
    host = [topo.host(c) for c in cores]
    chip = [topo.chip(c) for c in cores]
    tokens, fill = [], [0] * n
    for r in range(n):
        for t, e in enumerate(route[r]):
            tokens.append((r, t, e, fill[e]))
            fill[e] += 1
    via = choose_ways(tokens, cores, host, chip, topo)
    helper, relay = choose_cores(tokens, via, cores, host, chip, topo)

    plan = {}

    def prog(c):
        if c not in plan:
            plan[c] = {"blocks": [], "own": [], "pass": [], "handed": 0, "arrived": 0, "kept": [], "count": 0}
        return plan[c]

    for r in range(n):
        prog(cores[r])["count"] = fill[r]
    for (r, b), k in helper.items():
        prog(cores[r])["blocks"].append((b * BLOCK, k, b * BLOCK))
    for i, (r, t, e, p) in enumerate(tokens):
        if r == e:
            prog(cores[r])["kept"].append((t, p))
            continue
        mine = prog(helper[(r, t // BLOCK)])["own"]
        if i in relay:
            passing = prog(relay[i])["pass"]
            mine.append((t, relay[i], len(passing)))
            passing.append((len(passing), cores[e], p))
        else:
            mine.append((t, cores[e], p))
    for c in list(plan):
        for kind, engines, sem in (("blocks", 16, "handed"), ("own", 8, "arrived"), ("pass", 8, "arrived")):
            for call in pack(plan[c][kind], engines):
                for (slot, dst, dslot), per, mask in call:
                    plan[dst][sem] += per
    return plan


def send(g, core, T, topo, sends, engines, src, dst, sem, width):
    total = 0
    for call in pack(sends, engines):
        transfers = []
        for (slot, to, dslot), per, mask in call:
            rid, pid = topo.addr(to, core)
            transfers.append(RemoteDMATransfer(
                dst_ids=[DstId(rid=rid, pnc=pid)], dma_engine_mask=mask, remote_sem=sem,
                src=src[:, slot:slot + width, :], dst=dst[:, dslot:dslot + width, :]))
            total += per
        g.remote_dma_fused(transfers, local_sem=T.sem.read)
    return total


def rank_program(g, core, T, topo):
    if "plan" not in PLANS:
        PLANS["plan"] = build_plan(T.tables["ROUTE"], list(T.cores), topo)
    me = PLANS["plan"].get(core)
    if me is None:
        return
    if T.rank_of(core) is None:
        left = 0
        if me["own"]:
            g.wait_ge(T.sem.handed, me["handed"])
            left += send(g, core, T, topo, me["own"], 8, T.xs, T.land, T.sem.arrived, 1)
        if me["pass"]:
            g.wait_ge(T.sem.arrived, me["arrived"])
            left += send(g, core, T, topo, me["pass"], 8, T.land, T.land, T.sem.arrived, 1)
        g.wait_ge(T.sem.read, left)
        return
    g.dma_start(T.xs[:], T.x[:]).then_inc(T.sem.loaded, 16)
    g.wait_ge(T.sem.loaded, 16)
    left = send(g, core, T, topo, me["blocks"], 16, T.xs, T.xs, T.sem.handed, BLOCK)
    runs = spaced_runs(me["kept"])
    for t, step, m, p in runs:
        g.dma_start(T.land[:, p:p + m, :], T.xs[:, t:t + step * (m - 1) + 1:step, :]).then_inc(T.sem.kept, 16)
    g.wait_ge(T.sem.arrived, me["arrived"])
    if runs:
        g.wait_ge(T.sem.kept, 16 * len(runs))
    g.dma_start(T.y[:, :me["count"] * T.tables["W"]], T.land[:, :me["count"], :]).then_inc(T.sem.stored, 16)
    g.wait_ge(T.sem.stored, 16)
    g.wait_ge(T.sem.read, left)
